import numpy as np
import ml_dtypes


def mxq(x, axis, fmt="e4m3"):
    dtype, down = {"e4m3": (ml_dtypes.float8_e4m3fn, 7), "e5m2": (ml_dtypes.float8_e5m2, 14)}[fmt]
    v = np.moveaxis(np.asarray(x, np.float32).astype(ml_dtypes.bfloat16).astype(np.float64), axis, -1)
    blocks = v.reshape(v.shape[:-1] + (-1, 32))
    amax = np.abs(blocks).max(-1, keepdims=True)
    byte = np.maximum(np.where(amax > 0, np.frexp(amax)[1] - 1 + 127, 0) - down, 1)
    scale = np.exp2(byte - 127.0)
    codes = (blocks / scale).astype(np.float32).astype(dtype).astype(np.float64)
    return np.moveaxis((codes * scale).reshape(v.shape), -1, axis)


WIDE = False


def mx_kscale(k):
    if not WIDE:
        return np.ones(k)
    levels = np.array([10, -10, 5, -5, 0])
    if k % 512:
        return np.exp2(np.random.permutation(np.resize(levels, k // 32))).repeat(32)
    a = np.empty((k // 512, 16))
    for p in range(k // 512):
        a[p, :8] = np.random.permutation(np.resize(levels, 8))
        for g in range(8):
            far = levels[np.abs(levels - a[p, g]) >= 10]
            a[p, g + 8] = far[np.random.randint(len(far))]
    return np.exp2(a.ravel()).repeat(32)


BF16 = ml_dtypes.bfloat16


def bf(x):
    return np.asarray(x, np.float32).astype(BF16)


def f64(x):
    return np.asarray(x).astype(np.float64)


B, H, C = 512, 512, 8
HC = C * H


def draw0():
    s = mx_kscale(H)
    return {"z0": bf(np.random.standard_normal((B, H))),
            "g": bf((1.0 + 0.1 * np.random.standard_normal(H)) * s),
            "w": bf(np.random.standard_normal((H, HC)) / np.sqrt(H) / s[:, None]),
            "dx0": bf(np.random.standard_normal((B, C)) * np.sqrt(2.0 / C)),
            "dxm": bf(np.random.standard_normal((B, C)) * np.sqrt(2.0 / C))}


def vector_field(z, g, wq, channels):
    batch, hidden = z.shape
    u = z * g[None, :]
    f = np.tanh(mxq(u, 1, "e4m3") @ wq)
    return f.reshape(batch, channels, hidden)


def apply_control(f, dx):
    return np.sum(f * dx[:, :, None], axis=1)


def core(z0, g, w, dx0, dxm):
    z0, g, dx0, dxm = f64(z0), f64(g), f64(dx0), f64(dxm)
    channels = dx0.shape[1]
    wq = mxq(f64(w), 0, "e4m3")
    f0 = vector_field(z0, g, wq, channels)
    zmid = z0 + apply_control(f0, dx0)
    f1 = vector_field(zmid, g, wq, channels)
    return apply_control(f1, dxm)


def e4m3fn_bytes(y):
    return np.clip(np.asarray(y, np.float64), -448.0, 448.0).astype(np.float32).astype(ml_dtypes.float8_e4m3fn).view(np.uint8)


def e4m3fn_values(b):
    return np.asarray(b, np.uint8).view(ml_dtypes.float8_e4m3fn).astype(np.float64)


def setup_inputs():
    d = draw0()
    x0 = np.asarray(d['w']).astype(np.float64)
    s = (np.max(np.abs(x0), axis=(1,), keepdims=True) / 448.0).astype(np.float32)
    out = {}
    for k, v in d.items():
        if k == 'w':
            out['w_bytes'] = e4m3fn_bytes(x0 / s.astype(np.float64))
            out['w_scale'] = s
        else:
            out[k] = v
    return out


def reference(z0, g, w_bytes, w_scale, dx0, dxm):
    return core(z0, g, e4m3fn_values(w_bytes) * w_scale.astype(np.float64), dx0, dxm)

@@ -1,0 +1,301 @@
+from contextlib import ExitStack
+
+import concourse.mybir as mybir
+from concourse.masks import make_identity
+
+F32 = mybir.dt.float32
+BF16 = mybir.dt.bfloat16
+U32 = mybir.dt.uint32
+U8 = mybir.dt.uint8
+FP8 = mybir.dt.float8_e4m3fn
+FP8X4 = mybir.dt.float8_e4m3fn_x4
+TANH = mybir.ActivationFunctionType.Tanh
+COPY = mybir.ActivationFunctionType.Copy
+MULT = mybir.AluOpType.mult
+ADD = mybir.AluOpType.add
+
+P = 128
+PACK = 4
+B, H, C = 512, 512, 8
+NB = B // P
+
+FLOPS = 2 * 2 * B * H * C * H
+
+DIAG = (2, 1)
+JOIN = 7
+MM_BANKS = 4
+F_TILES = 24
+C_MAJOR = 4
+WIDEN_V = (4, 0, 1, 2, 2, 3, 1, 0)
+DIAG_FROM, DIAG_STEP = 7, 1
+TURN_AT = (27, 30, 37, 37)
+SLOTS = (4, 3, 2, 2)
+PROD_AFTER = 4
+STAGGER = 12
+GAIN_LAG = (7, 6, 10, 9)
+
+
+def tile_neuralcdemidpointstep_kernel(tc, z0, g, w_bytes, w_scale, dx0, dxm, out):
+    nc = tc.nc
+    with ExitStack() as ctx:
+        keep = ctx.enter_context(tc.tile_pool(name="keep", bufs=1))
+        work = ctx.enter_context(tc.tile_pool(name="work", bufs=3))
+        psum = ctx.enter_context(tc.psum_pool(name="psum", bufs=1))
+        ctx.enter_context(tc.manual_schedule())
+
+        s4 = keep.tile([P, PACK], F32, name="s4")
+        g4 = keep.tile([P, PACK], BF16, name="g4")
+        dxs = [keep.tile([P, NB, C], BF16, name="dx0_sb"), keep.tile([P, NB, C], BF16, name="dxm_sb")]
+        dxf = [keep.tile([P, NB, C], F32, name="dx0_f"), keep.tile([P, NB, C], F32, name="dxm_f")]
+        z_sb = keep.tile([P, NB, H], BF16, name="z_sb")
+        wb_tiles = [keep.tile([P, PACK, H], U8, name="wb0"), keep.tile([P, PACK, H], U8, name="wb1")]
+        wb_pairs = [keep.tile([P, PACK, 2 * H], U8, name="wb23"), keep.tile([P, PACK, 2 * H], U8, name="wb45"),
+                    keep.tile([P, PACK, 2 * H], U8, name="wb67")]
+        w_view = w_bytes.rearrange("(p t) n -> p t n", t=PACK)
+        z_view = z0.rearrange("(q p) h -> p q h", p=P)
+
+        nc.scalar.dma_start(out=s4[:], in_=w_scale.rearrange("(p t) o -> p (t o)", t=PACK))
+        nc.sync.dma_start(out=wb_tiles[0][:], in_=w_view[:, :, 0:H])
+        nc.sync.dma_start(out=z_sb[:, 0:2, :], in_=z_view[:, 0:2, :])
+        nc.sync.dma_start(out=wb_tiles[1][:], in_=w_view[:, :, H:2 * H])
+        nc.sync.dma_start(out=z_sb[:, 2:4, :], in_=z_view[:, 2:4, :])
+        nc.scalar.dma_start(out=g4[:], in_=g.rearrange("(p t) -> p t", t=PACK))
+        nc.scalar.dma_start(out=dxs[0][:], in_=dx0.rearrange("(q p) c -> p q c", p=P))
+        nc.scalar.dma_start(out=dxs[1][:], in_=dxm.rearrange("(q p) c -> p q c", p=P))
+        for j in range(3):
+            nc.sync.dma_start(out=wb_pairs[j][:], in_=w_view[:, :, (2 + 2 * j) * H:(4 + 2 * j) * H])
+
+        def w_codes_in(c, t):
+            if c < 2:
+                return wb_tiles[c][:, t, :]
+            return wb_pairs[c // 2 - 1][:, t, (c % 2) * H:(c % 2 + 1) * H]
+
+        warm = keep.tile([P, 1], F32, name="warm")
+        nc.gpsimd.memset(warm[:], 0.0)
+        nc.scalar.activation(out=warm[:], in_=warm[:], func=TANH)
+        ident = keep.tile([P, P], F32, name="ident")
+        make_identity(nc, ident[:])
+        ident_bf = keep.tile([P, P], BF16, name="ident_bf")
+        nc.gpsimd.tensor_copy(out=ident_bf[:], in_=ident[:])
+
+        w_codes = [keep.tile([P, H], U32, name=f"w_codes{c}", align_bytes=64) for c in range(C)]
+        w_scales = [keep.tile([P, H], U8, name=f"w_scales{c}", align_bytes=64) for c in range(C)]
+        u_codes = [[keep.tile([P, P], U32, name=f"u_codes{s}{b}", align_bytes=64) for b in range(NB)] for s in range(2)]
+        u_scales = [[keep.tile([P, P], U8, name=f"u_scales{s}{b}", align_bytes=64) for b in range(NB)] for s in range(2)]
+        prods = [keep.tile([P, SLOTS[b], H], F32, name=f"prods{b}") for b in range(NB)]
+        slots_used = [set() for b in range(NB)]
+        wide = [keep.tile([P, PACK, H], BF16, name=f"wide{c}") for c in range(C)]
+        grouped = {}
+        acc_ps = {}
+        zsum = {}
+        turned = {}
+        f_sb = {}
+        un = {}
+        accs = {}
+        diag = {}
+
+        for s in range(2):
+            nc.gpsimd.tensor_copy(out=dxf[s][:], in_=dxs[s][:])
+            for c in range(DIAG[s]):
+                for b in range(NB):
+                    diag[s, b, c] = keep.tile([P, P], F32, name=f"diag{s}{b}{c}")
+                    nc.gpsimd.tensor_scalar(out=diag[s, b, c][:], in0=ident[:], scalar1=dxf[s][:, b, c:c + 1], scalar2=0.0,
+                                            op0=MULT, op1=ADD)
+
+        def widen_s(c, t):
+            nc.scalar.activation(out=wide[c][:, t, :], in_=w_codes_in(c, t).bitcast(FP8), func=COPY, scale=s4[:, t:t + 1])
+
+        def widen_v(c, t):
+            nc.vector.tensor_scalar(out=wide[c][:, t, :], in0=w_codes_in(c, t).bitcast(FP8), scalar1=s4[:, t:t + 1],
+                                    scalar2=None, op0=MULT)
+
+        def interleave(c):
+            grouped[c] = work.tile([P, H, PACK], BF16, name="grouped", bufs=3, align_bytes=64)
+            nc.vector.tensor_copy(out=grouped[c][:].rearrange("p (n i) t -> p n t i", i=4),
+                                  in_=wide[c][:].rearrange("p t (n i) -> p n t i", i=4))
+
+        def quant_w(c):
+            nc.vector.quantize_mx(out=w_codes[c][:].bitcast(FP8X4), scales=w_scales[c][:],
+                                  in_=grouped[c][:].rearrange("p n t -> p (n t)"))
+
+        def quant_u(s, b):
+            nc.vector.quantize_mx(out=u_codes[s][b][:].bitcast(FP8X4), scales=u_scales[s][b][:],
+                                  in_=un[s, b][:].rearrange("p n t -> p (n t)"))
+
+        def gain(s, b):
+            un[s, b] = work.tile([P, P, PACK], BF16, name="un", bufs=4, align_bytes=64)
+            if s == 0:
+                nc.vector.tensor_tensor(
+                    out=un[s, b][:].rearrange("p n (u e) -> p n u e", u=2),
+                    in0=turned[s, b][:].bitcast(BF16).rearrange("p u (n e) -> p n u e", e=2),
+                    in1=g4[:].rearrange("p (u e) -> p u e", u=2).unsqueeze(1).to_broadcast([P, P, 2, 2]), op=MULT)
+            else:
+                nc.vector.tensor_tensor(out=un[s, b][:], in0=turned[s, b][:].rearrange("p t n -> p n t"),
+                                        in1=g4[:].unsqueeze(1).to_broadcast([P, P, PACK]), op=MULT)
+
+        def tanh(s, b, c):
+            f_sb[s, b, c] = work.tile([P, H], F32, name="f_sb", bufs=F_TILES)
+            src = acc_ps[s, b, c][:]
+            dst = f_sb[s, b, c][:]
+            if s == 0:
+                src = src.rearrange("p (m t) -> p t m", t=PACK)
+                dst = dst.rearrange("p (t m) -> p t m", t=PACK)
+            nc.scalar.activation(out=dst, in_=src, func=TANH)
+
+        def product(b, c):
+            slot = SLOTS[b] - 1 if c == JOIN else (c - DIAG[0]) % (SLOTS[b] - 1)
+            dst = prods[b][:, slot, :]
+            scalar = dxf[0][:, b, c:c + 1]
+            if c == JOIN:
+                nc.vector.scalar_tensor_tensor(out=dst, in0=f_sb[0, b, c][:], scalar=scalar, in1=zsum[0, b][:], op0=MULT, op1=ADD)
+            elif slot in slots_used[b]:
+                nc.vector.scalar_tensor_tensor(out=dst, in0=f_sb[0, b, c][:], scalar=scalar, in1=dst, op0=MULT, op1=ADD)
+            else:
+                nc.vector.tensor_scalar(out=dst, in0=f_sb[0, b, c][:], scalar1=scalar, scalar2=None, op0=MULT)
+            slots_used[b].add(slot)
+
+        def accumulate(b, c):
+            f = f_sb[1, b, c][:]
+            scalar = dxf[1][:, b, c:c + 1]
+            acc = work.tile([P, H], F32, name=f"acc{b % 2}", bufs=2)
+            prev = zsum[1, b] if c == DIAG[1] else accs[b] if c > 0 else None
+            if prev is None:
+                nc.vector.tensor_scalar(out=acc[:], in0=f, scalar1=scalar, scalar2=None, op0=MULT)
+            else:
+                nc.vector.scalar_tensor_tensor(out=acc[:], in0=f, scalar=scalar, in1=prev[:], op0=MULT, op1=ADD)
+            accs[b] = acc
+            if c == C - 1:
+                nc.sync.dma_start(out=out[b * P:(b + 1) * P, :], in_=acc[:])
+
+        def turn_z0(b):
+            turned[0, b] = psum.tile([P, 2, P], F32, name="mm", bufs=MM_BANKS)
+            words = z_sb[:, b, :].bitcast(F32)
+            for e in range(2):
+                nc.tensor.transpose(turned[0, b][:, e, :], words[:, e::2], ident[:])
+
+        def add_z0(b):
+            zsum[0, b] = psum.tile([P, H], F32, name="zs", bufs=4)
+            nc.tensor.matmul(zsum[0, b][:].rearrange("p (t m) -> p t m", t=PACK), lhsT=ident_bf[:],
+                             rhs=z_sb[:, b, :].rearrange("p (m t) -> p t m", t=PACK), start=True, stop=False)
+
+        def add_scaled(s, b, c):
+            if s == 1 and c == 0:
+                zsum[s, b] = psum.tile([P, H], F32, name="zs", bufs=4)
+            nc.tensor.matmul(zsum[s, b][:], lhsT=diag[s, b, c][:], rhs=f_sb[s, b, c][:], start=(s == 1 and c == 0),
+                             stop=(c == DIAG[s] - 1))
+
+        def turn(b, t):
+            if t == 0:
+                turned[1, b] = psum.tile([P, PACK, P], F32, name="zs", bufs=4)
+            for j in range(SLOTS[b]):
+                nc.tensor.matmul(turned[1, b][:, t, :], lhsT=prods[b][:, j, t * P:(t + 1) * P], rhs=ident[:], is_transpose=True,
+                                 start=(j == 0), stop=(j == SLOTS[b] - 1))
+
+        def mm(s, b, c):
+            acc_ps[s, b, c] = psum.tile([P, H], F32, name="mm", bufs=MM_BANKS)
+            nc.tensor.matmul_mx(out=acc_ps[s, b, c][:], lhsT=u_codes[s][b][:].bitcast(FP8X4), lhsT_scale=u_scales[s][b][:],
+                                rhs=w_codes[c][:].bitcast(FP8X4), rhs_scale=w_scales[c][:], start=True, stop=True)
+
+        units = [(0, b, c) for c in range(C_MAJOR) for b in range(NB)]
+        units += [(0, b, c) for b in range(NB) for c in range(C_MAJOR, C)]
+        late = sorted((16 * (b // 2) + 2 * c + STAGGER * (b % 2), b, c) for b in range(NB) for c in range(C))
+        units += [(1, b, c) for k, b, c in late]
+
+        widen_on_s = [(c, t) for c in range(C) for t in range(PACK - WIDEN_V[c])]
+        widen_on_v = [[(c, t) for t in range(PACK - WIDEN_V[c], PACK)] for c in range(C)]
+
+        scalar_q = [(widen_s, a) for a in widen_on_s[:6]]
+        rest = widen_on_s[6:]
+        for k, u in enumerate(units):
+            scalar_q.append((tanh, u))
+            if k < len(rest):
+                scalar_q.append((widen_s, rest[k]))
+
+        prod_order = [(b, c) for s, b, c in units[:NB * C] if c >= DIAG[0]]
+        vector_q = [(widen_v, a) for a in widen_on_v[0]]
+        vector_q += [(gain, (0, 0)), (interleave, (0,)), (quant_u, (0, 0)), (quant_w, (0,))]
+        for b in range(1, NB):
+            vector_q += [(gain, (0, b))]
+            if b == 1:
+                vector_q += [(widen_v, a) for a in widen_on_v[1]]
+                vector_q += [(interleave, (1,))]
+            vector_q += [(quant_u, (0, b))]
+        for c in range(1, C):
+            if c + 1 < C:
+                vector_q += [(widen_v, a) for a in widen_on_v[c + 1]]
+            vector_q += [(quant_w, (c,))]
+            if c + 1 < C:
+                vector_q += [(interleave, (c + 1,))]
+            if c >= PROD_AFTER:
+                vector_q += [(product, prod_order.pop(0)) for k in range(2)]
+        last = {}
+        tail_q = [(product, a) for a in prod_order]
+        for k, (b, c) in enumerate(prod_order):
+            last[b] = k
+        tail_q += [(accumulate, (b, c)) for s, b, c in units[NB * C:] if c >= DIAG[1]]
+        for k, op in enumerate(tail_q):
+            for b in range(NB):
+                if k == last[b] + GAIN_LAG[b]:
+                    vector_q.append((gain, (1, b)))
+                if k == last[b] + GAIN_LAG[b] + 1:
+                    vector_q.append((quant_u, (1, b)))
+            vector_q.append(op)
+
+        tensor_q = [(turn_z0, (b,)) for b in range(NB)] + [(add_z0, (b,)) for b in range(NB)]
+        adds = [(0, b, c) for c in range(DIAG[0]) for b in range(NB)]
+        turns = [(b, t) for b in range(NB) for t in range(PACK)]
+        for k, u in enumerate(units):
+            for b in range(NB):
+                if TURN_AT[b] <= k < TURN_AT[b] + PACK:
+                    tensor_q.append((turn, (b, k - TURN_AT[b])))
+            tensor_q.append((mm, u))
+            if k >= DIAG_FROM and (k - DIAG_FROM) % DIAG_STEP == 0 and adds:
+                tensor_q.append((add_scaled, adds.pop(0)))
+            j = k - MM_BANKS + 1
+            if j >= NB * C and units[j][2] < DIAG[1]:
+                tensor_q.append((add_scaled, units[j]))
+
+        issued = set()
+        order = {u: k for k, u in enumerate(units)}
+        f_reader = {}
+        for s, b, c in units:
+            f_reader[s, b, c] = (add_scaled, (s, b, c)) if c < DIAG[s] else (product, (b, c)) if s == 0 else (accumulate, (b, c))
+
+        def needs(fn, a):
+            if fn == interleave:
+                return [(widen_v if t >= PACK - WIDEN_V[a[0]] else widen_s, (a[0], t)) for t in range(PACK)]
+            if fn == quant_w:
+                return [(interleave, a)]
+            if fn == gain:
+                return [(turn_z0, (a[1],))] if a[0] == 0 else [(turn, (a[1], PACK - 1))]
+            if fn == quant_u:
+                return [(gain, a)]
+            if fn == mm:
+                k = order[a]
+                r = [(quant_u, a[:2]), (quant_w, a[2:])]
+                if k >= MM_BANKS:
+                    r.append((tanh, units[k - MM_BANKS]))
+                return r
+            if fn == tanh:
+                k = order[a]
+                return [(mm, a)] + ([f_reader[units[k - F_TILES]]] if k >= F_TILES else [])
+            if fn == product:
+                return [(tanh, (0,) + a)] + ([(add_scaled, (0, a[0], DIAG[0] - 1))] if a[1] == JOIN else [])
+            if fn == accumulate:
+                return [(tanh, (1,) + a)] + ([(add_scaled, (1, a[0], DIAG[1] - 1))] if a[1] == DIAG[1] and DIAG[1] else [])
+            if fn == add_scaled:
+                return [(tanh, a)]
+            if fn == turn:
+                return [(product, (a[0], c)) for c in range(DIAG[0], C)]
+            return []
+
+        queues = [tensor_q, scalar_q, vector_q]
+        while any(queues):
+            before = len(issued)
+            for q in queues:
+                while q and all(n in issued for n in needs(q[0][0], q[0][1])):
+                    fn, a = q.pop(0)
+                    fn(*a)
+                    issued.add((fn, a))
+            if len(issued) == before:
+                raise AssertionError(f"stuck: {[(str(q[0][0]).split('.')[2][:16], q[0][1], [(str(n[0]).split('.')[2][:16],n[1]) for n in needs(*q[0]) if n not in issued]) for q in queues if q]}")

@@ -21,18 +21,29 @@ NB = B // P
 
 FLOPS = 2 * 2 * B * H * C * H
 
-DIAG = (2, 1)
-JOIN = 7
-MM_BANKS = 4
+PEC = ((2, 3, 4, 0), (0, 0, 1, 2))
+MM_BANKS = 5
+ZS_BANKS = 8 - MM_BANKS
 F_TILES = 24
 C_MAJOR = 4
-WIDEN_V = (4, 0, 1, 2, 2, 3, 1, 0)
-DIAG_FROM, DIAG_STEP = 7, 1
-TURN_AT = (27, 30, 37, 37)
-SLOTS = (4, 3, 2, 2)
-PROD_AFTER = 4
-STAGGER = 12
-GAIN_LAG = (7, 6, 10, 9)
+WIDEN_V = (4, 0, 3, 1, 1, 1, 1, 1)
+HEAD_S = 8
+DIAG_HEAD = 16
+DIAG2_FROM = 19
+DIAG_FROM = 4
+DIAG_STEP = 2
+TURN_AT = (27, 31, 35, 41)
+TURN_GROUP = (4, 4, 4, 1)
+SLOTS = (5, 2, 4, 6)
+PROD_AFTER = 5
+PROD_RATE = 1
+STAGGER = 9
+CSTEP = 2
+OFF = 6
+LEAD = 2
+ADD_LAG = 1
+GAIN_LAG = (7, 7, 7, 13)
+FIRST_IL = 1
 
 
 def tile_neuralcdemidpointstep_kernel(tc, z0, g, w_bytes, w_scale, dx0, dxm, out):
@@ -54,13 +65,14 @@ def tile_neuralcdemidpointstep_kernel(tc, z0, g, w_bytes, w_scale, dx0, dxm, out
         w_view = w_bytes.rearrange("(p t) n -> p t n", t=PACK)
         z_view = z0.rearrange("(q p) h -> p q h", p=P)
 
+        nc.scalar.dma_start(out=dxs[0][:], in_=dx0.rearrange("(q p) c -> p q c", p=P))
         nc.scalar.dma_start(out=s4[:], in_=w_scale.rearrange("(p t) o -> p (t o)", t=PACK))
-        nc.sync.dma_start(out=wb_tiles[0][:], in_=w_view[:, :, 0:H])
+        for t in range(0, PACK, 2):
+            nc.sync.dma_start(out=wb_tiles[0][:, t:t + 2, :], in_=w_view[:, t:t + 2, 0:H])
         nc.sync.dma_start(out=z_sb[:, 0:2, :], in_=z_view[:, 0:2, :])
         nc.sync.dma_start(out=wb_tiles[1][:], in_=w_view[:, :, H:2 * H])
         nc.sync.dma_start(out=z_sb[:, 2:4, :], in_=z_view[:, 2:4, :])
         nc.scalar.dma_start(out=g4[:], in_=g.rearrange("(p t) -> p t", t=PACK))
-        nc.scalar.dma_start(out=dxs[0][:], in_=dx0.rearrange("(q p) c -> p q c", p=P))
         nc.scalar.dma_start(out=dxs[1][:], in_=dxm.rearrange("(q p) c -> p q c", p=P))
         for j in range(3):
             nc.sync.dma_start(out=wb_pairs[j][:], in_=w_view[:, :, (2 + 2 * j) * H:(4 + 2 * j) * H])
@@ -94,23 +106,34 @@ def tile_neuralcdemidpointstep_kernel(tc, z0, g, w_bytes, w_scale, dx0, dxm, out
         accs = {}
         diag = {}
 
-        for s in range(2):
-            nc.gpsimd.tensor_copy(out=dxf[s][:], in_=dxs[s][:])
-            for c in range(DIAG[s]):
-                for b in range(NB):
-                    diag[s, b, c] = keep.tile([P, P], F32, name=f"diag{s}{b}{c}")
-                    nc.gpsimd.tensor_scalar(out=diag[s, b, c][:], in0=ident[:], scalar1=dxf[s][:, b, c:c + 1], scalar2=0.0,
-                                            op0=MULT, op1=ADD)
+        def pieces(s, b, c):
+            if (s, b, c) == units[-1]:
+                return [slice(0, H // 2), slice(H // 2, H)]
+            return [slice(0, H)]
+
+        def spread(s):
+            nc.scalar.copy(out=dxf[s][:], in_=dxs[s][:])
+
+        def make_diag(s, b, c):
+            diag[s, b, c] = keep.tile([P, P], F32, name=f"diag{s}{b}{c}")
+            nc.scalar.activation(out=diag[s, b, c][:], in_=ident[:], func=COPY, scale=dxf[s][:, b, c:c + 1])
 
         def widen_s(c, t):
             nc.scalar.activation(out=wide[c][:, t, :], in_=w_codes_in(c, t).bitcast(FP8), func=COPY, scale=s4[:, t:t + 1])
 
         def widen_v(c, t):
-            nc.vector.tensor_scalar(out=wide[c][:, t, :], in0=w_codes_in(c, t).bitcast(FP8), scalar1=s4[:, t:t + 1],
+            dst = wide[c][:, t, :]
+            if WIDEN_V[c] == PACK:
+                dst = wide[c][:].rearrange("p (u x) n -> p u (x n)", u=2).rearrange("p u (n e) -> p u n e", e=2)[:, t // 2, :, t % 2]
+            nc.vector.tensor_scalar(out=dst, in0=w_codes_in(c, t).bitcast(FP8), scalar1=s4[:, t:t + 1],
                                     scalar2=None, op0=MULT)
 
         def interleave(c):
             grouped[c] = work.tile([P, H, PACK], BF16, name="grouped", bufs=3, align_bytes=64)
+            if WIDEN_V[c] == PACK:
+                words = wide[c][:].rearrange("p (u x) n -> p u (x n)", u=2).bitcast(F32)
+                nc.vector.tensor_copy(out=grouped[c][:].bitcast(F32), in_=words.rearrange("p u n -> p n u"))
+                return
             nc.vector.tensor_copy(out=grouped[c][:].rearrange("p (n i) t -> p n t i", i=4),
                                   in_=wide[c][:].rearrange("p t (n i) -> p n t i", i=4))
 
@@ -135,37 +158,45 @@ def tile_neuralcdemidpointstep_kernel(tc, z0, g, w_bytes, w_scale, dx0, dxm, out
 
         def tanh(s, b, c):
             f_sb[s, b, c] = work.tile([P, H], F32, name="f_sb", bufs=F_TILES)
-            src = acc_ps[s, b, c][:]
-            dst = f_sb[s, b, c][:]
-            if s == 0:
-                src = src.rearrange("p (m t) -> p t m", t=PACK)
-                dst = dst.rearrange("p (t m) -> p t m", t=PACK)
-            nc.scalar.activation(out=dst, in_=src, func=TANH)
+            for cols in pieces(s, b, c):
+                src = acc_ps[s, b, c][:, cols]
+                dst = f_sb[s, b, c][:, cols]
+                if s == 0:
+                    src = src.rearrange("p (m t) -> p t m", t=PACK)
+                    dst = dst.rearrange("p (t m) -> p t m", t=PACK)
+                nc.scalar.activation(out=dst, in_=src, func=TANH)
 
         def product(b, c):
-            slot = SLOTS[b] - 1 if c == JOIN else (c - DIAG[0]) % (SLOTS[b] - 1)
+            joins = c == C - 1 and PEC[0][b] > 0
+            plain = SLOTS[b] - (1 if PEC[0][b] > 0 else 0)
+            slot = SLOTS[b] - 1 if joins else (c - PEC[0][b]) % plain
             dst = prods[b][:, slot, :]
-            scalar = dxf[0][:, b, c:c + 1]
-            if c == JOIN:
-                nc.vector.scalar_tensor_tensor(out=dst, in0=f_sb[0, b, c][:], scalar=scalar, in1=zsum[0, b][:], op0=MULT, op1=ADD)
+            f = f_sb[0, b, c][:]
+            scalar = dxs[0][:, b, c:c + 1]
+            if joins:
+                nc.vector.scalar_tensor_tensor(out=dst, in0=f, scalar=scalar, in1=zsum[0, b][:], op0=MULT, op1=ADD)
             elif slot in slots_used[b]:
-                nc.vector.scalar_tensor_tensor(out=dst, in0=f_sb[0, b, c][:], scalar=scalar, in1=dst, op0=MULT, op1=ADD)
+                nc.vector.scalar_tensor_tensor(out=dst, in0=f, scalar=scalar, in1=dst, op0=MULT, op1=ADD)
+            elif PEC[0][b] == 0 and slot == 0:
+                nc.vector.scalar_tensor_tensor(out=dst.rearrange("p (t m) -> p t m", t=PACK), in0=f.rearrange("p (t m) -> p t m", t=PACK),
+                                               scalar=scalar, in1=z_sb[:, b, :].rearrange("p (m t) -> p t m", t=PACK), op0=MULT, op1=ADD)
             else:
-                nc.vector.tensor_scalar(out=dst, in0=f_sb[0, b, c][:], scalar1=scalar, scalar2=None, op0=MULT)
+                nc.vector.tensor_scalar(out=dst, in0=f, scalar1=scalar, scalar2=None, op0=MULT)
             slots_used[b].add(slot)
 
         def accumulate(b, c):
-            f = f_sb[1, b, c][:]
-            scalar = dxf[1][:, b, c:c + 1]
+            scalar = dxs[1][:, b, c:c + 1]
             acc = work.tile([P, H], F32, name=f"acc{b % 2}", bufs=2)
-            prev = zsum[1, b] if c == DIAG[1] else accs[b] if c > 0 else None
-            if prev is None:
-                nc.vector.tensor_scalar(out=acc[:], in0=f, scalar1=scalar, scalar2=None, op0=MULT)
-            else:
-                nc.vector.scalar_tensor_tensor(out=acc[:], in0=f, scalar=scalar, in1=prev[:], op0=MULT, op1=ADD)
+            prev = zsum[1, b] if c == PEC[1][b] and c > 0 else accs[b] if c > 0 else None
+            for cols in pieces(1, b, c):
+                f = f_sb[1, b, c][:, cols]
+                if prev is None:
+                    nc.vector.tensor_scalar(out=acc[:, cols], in0=f, scalar1=scalar, scalar2=None, op0=MULT)
+                else:
+                    nc.vector.scalar_tensor_tensor(out=acc[:, cols], in0=f, scalar=scalar, in1=prev[:, cols], op0=MULT, op1=ADD)
+                if c == C - 1:
+                    nc.sync.dma_start(out=out[b * P:(b + 1) * P, cols], in_=acc[:, cols])
             accs[b] = acc
-            if c == C - 1:
-                nc.sync.dma_start(out=out[b * P:(b + 1) * P, :], in_=acc[:])
 
         def turn_z0(b):
             turned[0, b] = psum.tile([P, 2, P], F32, name="mm", bufs=MM_BANKS)
@@ -174,19 +205,19 @@ def tile_neuralcdemidpointstep_kernel(tc, z0, g, w_bytes, w_scale, dx0, dxm, out
                 nc.tensor.transpose(turned[0, b][:, e, :], words[:, e::2], ident[:])
 
         def add_z0(b):
-            zsum[0, b] = psum.tile([P, H], F32, name="zs", bufs=4)
+            zsum[0, b] = psum.tile([P, H], F32, name="zs", bufs=ZS_BANKS)
             nc.tensor.matmul(zsum[0, b][:].rearrange("p (t m) -> p t m", t=PACK), lhsT=ident_bf[:],
                              rhs=z_sb[:, b, :].rearrange("p (m t) -> p t m", t=PACK), start=True, stop=False)
 
         def add_scaled(s, b, c):
-            if s == 1 and c == 0:
-                zsum[s, b] = psum.tile([P, H], F32, name="zs", bufs=4)
-            nc.tensor.matmul(zsum[s, b][:], lhsT=diag[s, b, c][:], rhs=f_sb[s, b, c][:], start=(s == 1 and c == 0),
-                             stop=(c == DIAG[s] - 1))
+            if c == 0 and s == 1:
+                zsum[s, b] = psum.tile([P, H], F32, name="zs", bufs=ZS_BANKS)
+            nc.tensor.matmul(zsum[s, b][:], lhsT=diag[s, b, c][:], rhs=f_sb[s, b, c][:], start=(c == 0 and s == 1),
+                             stop=(c == PEC[s][b] - 1))
 
         def turn(b, t):
             if t == 0:
-                turned[1, b] = psum.tile([P, PACK, P], F32, name="zs", bufs=4)
+                turned[1, b] = psum.tile([P, PACK, P], F32, name="zs", bufs=ZS_BANKS)
             for j in range(SLOTS[b]):
                 nc.tensor.matmul(turned[1, b][:, t, :], lhsT=prods[b][:, j, t * P:(t + 1) * P], rhs=ident[:], is_transpose=True,
                                  start=(j == 0), stop=(j == SLOTS[b] - 1))
@@ -198,22 +229,32 @@ def tile_neuralcdemidpointstep_kernel(tc, z0, g, w_bytes, w_scale, dx0, dxm, out
 
         units = [(0, b, c) for c in range(C_MAJOR) for b in range(NB)]
         units += [(0, b, c) for b in range(NB) for c in range(C_MAJOR, C)]
-        late = sorted((16 * (b // 2) + 2 * c + STAGGER * (b % 2), b, c) for b in range(NB) for c in range(C))
-        units += [(1, b, c) for k, b, c in late]
+        keyed = [(k, u) for k, u in enumerate(units)]
+        for b in range(NB):
+            for c in range(C):
+                k = NB * C + OFF + (8 * b + c if CSTEP == 1 else 16 * (b // 2) + STAGGER * (b % 2) + 2 * c)
+                keyed.append((k - LEAD - 0.5 if c < PEC[1][b] else k, (1, b, c)))
+        units = [u for k, u in sorted(keyed)]
 
         widen_on_s = [(c, t) for c in range(C) for t in range(PACK - WIDEN_V[c])]
         widen_on_v = [[(c, t) for t in range(PACK - WIDEN_V[c], PACK)] for c in range(C)]
 
-        scalar_q = [(widen_s, a) for a in widen_on_s[:6]]
-        rest = widen_on_s[6:]
+        diags = [(0, b, c) for c in range(C) for b in range(NB) if c < PEC[0][b]]
+        later_diags = [u for u in units if u[0] == 1 and u[2] < PEC[1][u[1]]]
+        scalar_q = [(spread, (0,))] + [(make_diag, a) for a in diags[:DIAG_HEAD]]
+        scalar_q += [(widen_s, a) for a in widen_on_s[:HEAD_S]]
+        scalar_q += [(make_diag, a) for a in diags[DIAG_HEAD:]] + [(spread, (1,))]
+        rest = widen_on_s[HEAD_S:]
         for k, u in enumerate(units):
             scalar_q.append((tanh, u))
             if k < len(rest):
                 scalar_q.append((widen_s, rest[k]))
+            if k >= DIAG2_FROM and later_diags:
+                scalar_q.append((make_diag, later_diags.pop(0)))
 
-        prod_order = [(b, c) for s, b, c in units[:NB * C] if c >= DIAG[0]]
+        prod_order = [(s, b, c) for s, b, c in units if c >= PEC[s][b]]
         vector_q = [(widen_v, a) for a in widen_on_v[0]]
-        vector_q += [(gain, (0, 0)), (interleave, (0,)), (quant_u, (0, 0)), (quant_w, (0,))]
+        vector_q += [(interleave, (0,)), (gain, (0, 0)), (quant_w, (0,)), (quant_u, (0, 0))] if FIRST_IL else [(gain, (0, 0)), (interleave, (0,)), (quant_u, (0, 0)), (quant_w, (0,))]
         for b in range(1, NB):
             vector_q += [(gain, (0, b))]
             if b == 1:
@@ -227,12 +268,11 @@ def tile_neuralcdemidpointstep_kernel(tc, z0, g, w_bytes, w_scale, dx0, dxm, out
             if c + 1 < C:
                 vector_q += [(interleave, (c + 1,))]
             if c >= PROD_AFTER:
-                vector_q += [(product, prod_order.pop(0)) for k in range(2)]
-        last = {}
-        tail_q = [(product, a) for a in prod_order]
-        for k, (b, c) in enumerate(prod_order):
-            last[b] = k
-        tail_q += [(accumulate, (b, c)) for s, b, c in units[NB * C:] if c >= DIAG[1]]
+                for k in range(PROD_RATE):
+                    if prod_order and prod_order[0][0] == 0:
+                        vector_q.append((product, prod_order.pop(0)[1:]))
+        last = {b: k for k, (s, b, c) in enumerate(prod_order) if s == 0}
+        tail_q = [(product if s == 0 else accumulate, (b, c)) for s, b, c in prod_order]
         for k, op in enumerate(tail_q):
             for b in range(NB):
                 if k == last[b] + GAIN_LAG[b]:
@@ -241,25 +281,28 @@ def tile_neuralcdemidpointstep_kernel(tc, z0, g, w_bytes, w_scale, dx0, dxm, out
                     vector_q.append((quant_u, (1, b)))
             vector_q.append(op)
 
-        tensor_q = [(turn_z0, (b,)) for b in range(NB)] + [(add_z0, (b,)) for b in range(NB)]
-        adds = [(0, b, c) for c in range(DIAG[0]) for b in range(NB)]
-        turns = [(b, t) for b in range(NB) for t in range(PACK)]
-        for k, u in enumerate(units):
+        tensor_q = [(turn_z0, (b,)) for b in range(NB)]
+        adds = [(0, b, c) for c in range(C) for b in range(NB) if c < PEC[0][b]]
+        for k in range(len(units) + 8):
             for b in range(NB):
-                if TURN_AT[b] <= k < TURN_AT[b] + PACK:
-                    tensor_q.append((turn, (b, k - TURN_AT[b])))
-            tensor_q.append((mm, u))
+                j = k - TURN_AT[b]
+                if 0 <= j < PACK // TURN_GROUP[b]:
+                    tensor_q += [(turn, (b, t)) for t in range(j * TURN_GROUP[b], (j + 1) * TURN_GROUP[b])]
+            if k < len(units):
+                tensor_q.append((mm, units[k]))
             if k >= DIAG_FROM and (k - DIAG_FROM) % DIAG_STEP == 0 and adds:
+                if adds[0][2] == 0:
+                    tensor_q.append((add_z0, adds[0][1:2]))
                 tensor_q.append((add_scaled, adds.pop(0)))
-            j = k - MM_BANKS + 1
-            if j >= NB * C and units[j][2] < DIAG[1]:
+            j = k - MM_BANKS + 1 - ADD_LAG
+            if 0 <= j < len(units) and units[j][0] == 1 and units[j][2] < PEC[1][units[j][1]]:
                 tensor_q.append((add_scaled, units[j]))
 
         issued = set()
         order = {u: k for k, u in enumerate(units)}
         f_reader = {}
         for s, b, c in units:
-            f_reader[s, b, c] = (add_scaled, (s, b, c)) if c < DIAG[s] else (product, (b, c)) if s == 0 else (accumulate, (b, c))
+            f_reader[s, b, c] = (add_scaled, (s, b, c)) if c < PEC[s][b] else (product, (b, c)) if s == 0 else (accumulate, (b, c))
 
         def needs(fn, a):
             if fn == interleave:
@@ -280,20 +323,37 @@ def tile_neuralcdemidpointstep_kernel(tc, z0, g, w_bytes, w_scale, dx0, dxm, out
                 k = order[a]
                 return [(mm, a)] + ([f_reader[units[k - F_TILES]]] if k >= F_TILES else [])
             if fn == product:
-                return [(tanh, (0,) + a)] + ([(add_scaled, (0, a[0], DIAG[0] - 1))] if a[1] == JOIN else [])
+                return [(tanh, (0,) + a)] + ([(add_scaled, (0, a[0], PEC[0][a[0]] - 1))] if a[1] == C - 1 and PEC[0][a[0]] else [])
             if fn == accumulate:
-                return [(tanh, (1,) + a)] + ([(add_scaled, (1, a[0], DIAG[1] - 1))] if a[1] == DIAG[1] and DIAG[1] else [])
+                return [(tanh, (1,) + a)] + ([(add_scaled, (1, a[0], a[1] - 1))] if a[1] == PEC[1][a[0]] and a[1] else [])
             if fn == add_scaled:
-                return [(tanh, a)]
+                return [(tanh, a), (make_diag, a)]
             if fn == turn:
-                return [(product, (a[0], c)) for c in range(DIAG[0], C)]
+                return [(product, (a[0], c)) for c in range(PEC[0][a[0]], C)]
             return []
+
+        zs_readers = []
+
+        def bank_free(fn, a):
+            reader = None
+            if fn == add_z0:
+                reader = (product, (a[0], C - 1))
+            if fn == add_scaled and a[0] == 1 and a[2] == 0:
+                reader = (accumulate, (a[1], PEC[1][a[1]]))
+            if fn == turn and a[1] == 0:
+                reader = (gain, (1, a[0]))
+            if reader is None:
+                return True
+            if len(zs_readers) >= ZS_BANKS and zs_readers[-ZS_BANKS] not in issued:
+                return False
+            zs_readers.append(reader)
+            return True
 
         queues = [tensor_q, scalar_q, vector_q]
         while any(queues):
             before = len(issued)
             for q in queues:
-                while q and all(n in issued for n in needs(q[0][0], q[0][1])):
+                while q and all(n in issued for n in needs(q[0][0], q[0][1])) and bank_free(*q[0]):
                     fn, a = q.pop(0)
                     fn(*a)
                     issued.add((fn, a))

from contextlib import ExitStack

import concourse.mybir as mybir
from concourse.masks import make_identity

F32 = mybir.dt.float32
BF16 = mybir.dt.bfloat16
U32 = mybir.dt.uint32
U8 = mybir.dt.uint8
FP8 = mybir.dt.float8_e4m3fn
FP8X4 = mybir.dt.float8_e4m3fn_x4
TANH = mybir.ActivationFunctionType.Tanh
COPY = mybir.ActivationFunctionType.Copy
MULT = mybir.AluOpType.mult
ADD = mybir.AluOpType.add

P = 128
PACK = 4
B, H, C = 512, 512, 8
NB = B // P

FLOPS = 2 * 2 * B * H * C * H

PEC = ((2, 3, 4, 0), (0, 0, 1, 2))
MM_BANKS = 5
ZS_BANKS = 8 - MM_BANKS
F_TILES = 24
C_MAJOR = 4
WIDEN_V = (4, 0, 3, 1, 1, 1, 1, 1)
HEAD_S = 8
DIAG_HEAD = 16
DIAG2_FROM = 19
DIAG_FROM = 4
DIAG_STEP = 2
TURN_AT = (27, 31, 35, 41)
TURN_GROUP = (4, 4, 4, 1)
SLOTS = (5, 2, 4, 6)
PROD_AFTER = 5
PROD_RATE = 1
STAGGER = 9
CSTEP = 2
OFF = 6
LEAD = 2
ADD_LAG = 1
GAIN_LAG = (7, 7, 7, 13)
FIRST_IL = 1


def tile_neuralcdemidpointstep_kernel(tc, z0, g, w_bytes, w_scale, dx0, dxm, out):
    nc = tc.nc
    with ExitStack() as ctx:
        keep = ctx.enter_context(tc.tile_pool(name="keep", bufs=1))
        work = ctx.enter_context(tc.tile_pool(name="work", bufs=3))
        psum = ctx.enter_context(tc.psum_pool(name="psum", bufs=1))
        ctx.enter_context(tc.manual_schedule())

        s4 = keep.tile([P, PACK], F32, name="s4")
        g4 = keep.tile([P, PACK], BF16, name="g4")
        dxs = [keep.tile([P, NB, C], BF16, name="dx0_sb"), keep.tile([P, NB, C], BF16, name="dxm_sb")]
        dxf = [keep.tile([P, NB, C], F32, name="dx0_f"), keep.tile([P, NB, C], F32, name="dxm_f")]
        z_sb = keep.tile([P, NB, H], BF16, name="z_sb")
        wb_tiles = [keep.tile([P, PACK, H], U8, name="wb0"), keep.tile([P, PACK, H], U8, name="wb1")]
        wb_pairs = [keep.tile([P, PACK, 2 * H], U8, name="wb23"), keep.tile([P, PACK, 2 * H], U8, name="wb45"),
                    keep.tile([P, PACK, 2 * H], U8, name="wb67")]
        w_view = w_bytes.rearrange("(p t) n -> p t n", t=PACK)
        z_view = z0.rearrange("(q p) h -> p q h", p=P)

        nc.scalar.dma_start(out=dxs[0][:], in_=dx0.rearrange("(q p) c -> p q c", p=P))
        nc.scalar.dma_start(out=s4[:], in_=w_scale.rearrange("(p t) o -> p (t o)", t=PACK))
        for t in range(0, PACK, 2):
            nc.sync.dma_start(out=wb_tiles[0][:, t:t + 2, :], in_=w_view[:, t:t + 2, 0:H])
        nc.sync.dma_start(out=z_sb[:, 0:2, :], in_=z_view[:, 0:2, :])
        nc.sync.dma_start(out=wb_tiles[1][:], in_=w_view[:, :, H:2 * H])
        nc.sync.dma_start(out=z_sb[:, 2:4, :], in_=z_view[:, 2:4, :])
        nc.scalar.dma_start(out=g4[:], in_=g.rearrange("(p t) -> p t", t=PACK))
        nc.scalar.dma_start(out=dxs[1][:], in_=dxm.rearrange("(q p) c -> p q c", p=P))
        for j in range(3):
            nc.sync.dma_start(out=wb_pairs[j][:], in_=w_view[:, :, (2 + 2 * j) * H:(4 + 2 * j) * H])

        def w_codes_in(c, t):
            if c < 2:
                return wb_tiles[c][:, t, :]
            return wb_pairs[c // 2 - 1][:, t, (c % 2) * H:(c % 2 + 1) * H]

        warm = keep.tile([P, 1], F32, name="warm")
        nc.gpsimd.memset(warm[:], 0.0)
        nc.scalar.activation(out=warm[:], in_=warm[:], func=TANH)
        ident = keep.tile([P, P], F32, name="ident")
        make_identity(nc, ident[:])
        ident_bf = keep.tile([P, P], BF16, name="ident_bf")
        nc.gpsimd.tensor_copy(out=ident_bf[:], in_=ident[:])

        w_codes = [keep.tile([P, H], U32, name=f"w_codes{c}", align_bytes=64) for c in range(C)]
        w_scales = [keep.tile([P, H], U8, name=f"w_scales{c}", align_bytes=64) for c in range(C)]
        u_codes = [[keep.tile([P, P], U32, name=f"u_codes{s}{b}", align_bytes=64) for b in range(NB)] for s in range(2)]
        u_scales = [[keep.tile([P, P], U8, name=f"u_scales{s}{b}", align_bytes=64) for b in range(NB)] for s in range(2)]
        prods = [keep.tile([P, SLOTS[b], H], F32, name=f"prods{b}") for b in range(NB)]
        slots_used = [set() for b in range(NB)]
        wide = [keep.tile([P, PACK, H], BF16, name=f"wide{c}") for c in range(C)]
        grouped = {}
        acc_ps = {}
        zsum = {}
        turned = {}
        f_sb = {}
        un = {}
        accs = {}
        diag = {}

        def pieces(s, b, c):
            if (s, b, c) == units[-1]:
                return [slice(0, H // 2), slice(H // 2, H)]
            return [slice(0, H)]

        def spread(s):
            nc.scalar.copy(out=dxf[s][:], in_=dxs[s][:])

        def make_diag(s, b, c):
            diag[s, b, c] = keep.tile([P, P], F32, name=f"diag{s}{b}{c}")
            nc.scalar.activation(out=diag[s, b, c][:], in_=ident[:], func=COPY, scale=dxf[s][:, b, c:c + 1])

        def widen_s(c, t):
            nc.scalar.activation(out=wide[c][:, t, :], in_=w_codes_in(c, t).bitcast(FP8), func=COPY, scale=s4[:, t:t + 1])

        def widen_v(c, t):
            dst = wide[c][:, t, :]
            if WIDEN_V[c] == PACK:
                dst = wide[c][:].rearrange("p (u x) n -> p u (x n)", u=2).rearrange("p u (n e) -> p u n e", e=2)[:, t // 2, :, t % 2]
            nc.vector.tensor_scalar(out=dst, in0=w_codes_in(c, t).bitcast(FP8), scalar1=s4[:, t:t + 1],
                                    scalar2=None, op0=MULT)

        def interleave(c):
            grouped[c] = work.tile([P, H, PACK], BF16, name="grouped", bufs=3, align_bytes=64)
            if WIDEN_V[c] == PACK:
                words = wide[c][:].rearrange("p (u x) n -> p u (x n)", u=2).bitcast(F32)
                nc.vector.tensor_copy(out=grouped[c][:].bitcast(F32), in_=words.rearrange("p u n -> p n u"))
                return
            nc.vector.tensor_copy(out=grouped[c][:].rearrange("p (n i) t -> p n t i", i=4),
                                  in_=wide[c][:].rearrange("p t (n i) -> p n t i", i=4))

        def quant_w(c):
            nc.vector.quantize_mx(out=w_codes[c][:].bitcast(FP8X4), scales=w_scales[c][:],
                                  in_=grouped[c][:].rearrange("p n t -> p (n t)"))

        def quant_u(s, b):
            nc.vector.quantize_mx(out=u_codes[s][b][:].bitcast(FP8X4), scales=u_scales[s][b][:],
                                  in_=un[s, b][:].rearrange("p n t -> p (n t)"))

        def gain(s, b):
            un[s, b] = work.tile([P, P, PACK], BF16, name="un", bufs=4, align_bytes=64)
            if s == 0:
                nc.vector.tensor_tensor(
                    out=un[s, b][:].rearrange("p n (u e) -> p n u e", u=2),
                    in0=turned[s, b][:].bitcast(BF16).rearrange("p u (n e) -> p n u e", e=2),
                    in1=g4[:].rearrange("p (u e) -> p u e", u=2).unsqueeze(1).to_broadcast([P, P, 2, 2]), op=MULT)
            else:
                nc.vector.tensor_tensor(out=un[s, b][:], in0=turned[s, b][:].rearrange("p t n -> p n t"),
                                        in1=g4[:].unsqueeze(1).to_broadcast([P, P, PACK]), op=MULT)

        def tanh(s, b, c):
            f_sb[s, b, c] = work.tile([P, H], F32, name="f_sb", bufs=F_TILES)
            for cols in pieces(s, b, c):
                src = acc_ps[s, b, c][:, cols]
                dst = f_sb[s, b, c][:, cols]
                if s == 0:
                    src = src.rearrange("p (m t) -> p t m", t=PACK)
                    dst = dst.rearrange("p (t m) -> p t m", t=PACK)
                nc.scalar.activation(out=dst, in_=src, func=TANH)

        def product(b, c):
            joins = c == C - 1 and PEC[0][b] > 0
            plain = SLOTS[b] - (1 if PEC[0][b] > 0 else 0)
            slot = SLOTS[b] - 1 if joins else (c - PEC[0][b]) % plain
            dst = prods[b][:, slot, :]
            f = f_sb[0, b, c][:]
            scalar = dxs[0][:, b, c:c + 1]
            if joins:
                nc.vector.scalar_tensor_tensor(out=dst, in0=f, scalar=scalar, in1=zsum[0, b][:], op0=MULT, op1=ADD)
            elif slot in slots_used[b]:
                nc.vector.scalar_tensor_tensor(out=dst, in0=f, scalar=scalar, in1=dst, op0=MULT, op1=ADD)
            elif PEC[0][b] == 0 and slot == 0:
                nc.vector.scalar_tensor_tensor(out=dst.rearrange("p (t m) -> p t m", t=PACK), in0=f.rearrange("p (t m) -> p t m", t=PACK),
                                               scalar=scalar, in1=z_sb[:, b, :].rearrange("p (m t) -> p t m", t=PACK), op0=MULT, op1=ADD)
            else:
                nc.vector.tensor_scalar(out=dst, in0=f, scalar1=scalar, scalar2=None, op0=MULT)
            slots_used[b].add(slot)

        def accumulate(b, c):
            scalar = dxs[1][:, b, c:c + 1]
            acc = work.tile([P, H], F32, name=f"acc{b % 2}", bufs=2)
            prev = zsum[1, b] if c == PEC[1][b] and c > 0 else accs[b] if c > 0 else None
            for cols in pieces(1, b, c):
                f = f_sb[1, b, c][:, cols]
                if prev is None:
                    nc.vector.tensor_scalar(out=acc[:, cols], in0=f, scalar1=scalar, scalar2=None, op0=MULT)
                else:
                    nc.vector.scalar_tensor_tensor(out=acc[:, cols], in0=f, scalar=scalar, in1=prev[:, cols], op0=MULT, op1=ADD)
                if c == C - 1:
                    nc.sync.dma_start(out=out[b * P:(b + 1) * P, cols], in_=acc[:, cols])
            accs[b] = acc

        def turn_z0(b):
            turned[0, b] = psum.tile([P, 2, P], F32, name="mm", bufs=MM_BANKS)
            words = z_sb[:, b, :].bitcast(F32)
            for e in range(2):
                nc.tensor.transpose(turned[0, b][:, e, :], words[:, e::2], ident[:])

        def add_z0(b):
            zsum[0, b] = psum.tile([P, H], F32, name="zs", bufs=ZS_BANKS)
            nc.tensor.matmul(zsum[0, b][:].rearrange("p (t m) -> p t m", t=PACK), lhsT=ident_bf[:],
                             rhs=z_sb[:, b, :].rearrange("p (m t) -> p t m", t=PACK), start=True, stop=False)

        def add_scaled(s, b, c):
            if c == 0 and s == 1:
                zsum[s, b] = psum.tile([P, H], F32, name="zs", bufs=ZS_BANKS)
            nc.tensor.matmul(zsum[s, b][:], lhsT=diag[s, b, c][:], rhs=f_sb[s, b, c][:], start=(c == 0 and s == 1),
                             stop=(c == PEC[s][b] - 1))

        def turn(b, t):
            if t == 0:
                turned[1, b] = psum.tile([P, PACK, P], F32, name="zs", bufs=ZS_BANKS)
            for j in range(SLOTS[b]):
                nc.tensor.matmul(turned[1, b][:, t, :], lhsT=prods[b][:, j, t * P:(t + 1) * P], rhs=ident[:], is_transpose=True,
                                 start=(j == 0), stop=(j == SLOTS[b] - 1))

        def mm(s, b, c):
            acc_ps[s, b, c] = psum.tile([P, H], F32, name="mm", bufs=MM_BANKS)
            nc.tensor.matmul_mx(out=acc_ps[s, b, c][:], lhsT=u_codes[s][b][:].bitcast(FP8X4), lhsT_scale=u_scales[s][b][:],
                                rhs=w_codes[c][:].bitcast(FP8X4), rhs_scale=w_scales[c][:], start=True, stop=True)

        units = [(0, b, c) for c in range(C_MAJOR) for b in range(NB)]
        units += [(0, b, c) for b in range(NB) for c in range(C_MAJOR, C)]
        keyed = [(k, u) for k, u in enumerate(units)]
        for b in range(NB):
            for c in range(C):
                k = NB * C + OFF + (8 * b + c if CSTEP == 1 else 16 * (b // 2) + STAGGER * (b % 2) + 2 * c)
                keyed.append((k - LEAD - 0.5 if c < PEC[1][b] else k, (1, b, c)))
        units = [u for k, u in sorted(keyed)]

        widen_on_s = [(c, t) for c in range(C) for t in range(PACK - WIDEN_V[c])]
        widen_on_v = [[(c, t) for t in range(PACK - WIDEN_V[c], PACK)] for c in range(C)]

        diags = [(0, b, c) for c in range(C) for b in range(NB) if c < PEC[0][b]]
        later_diags = [u for u in units if u[0] == 1 and u[2] < PEC[1][u[1]]]
        scalar_q = [(spread, (0,))] + [(make_diag, a) for a in diags[:DIAG_HEAD]]
        scalar_q += [(widen_s, a) for a in widen_on_s[:HEAD_S]]
        scalar_q += [(make_diag, a) for a in diags[DIAG_HEAD:]] + [(spread, (1,))]
        rest = widen_on_s[HEAD_S:]
        for k, u in enumerate(units):
            scalar_q.append((tanh, u))
            if k < len(rest):
                scalar_q.append((widen_s, rest[k]))
            if k >= DIAG2_FROM and later_diags:
                scalar_q.append((make_diag, later_diags.pop(0)))

        prod_order = [(s, b, c) for s, b, c in units if c >= PEC[s][b]]
        vector_q = [(widen_v, a) for a in widen_on_v[0]]
        vector_q += [(interleave, (0,)), (gain, (0, 0)), (quant_w, (0,)), (quant_u, (0, 0))] if FIRST_IL else [(gain, (0, 0)), (interleave, (0,)), (quant_u, (0, 0)), (quant_w, (0,))]
        for b in range(1, NB):
            vector_q += [(gain, (0, b))]
            if b == 1:
                vector_q += [(widen_v, a) for a in widen_on_v[1]]
                vector_q += [(interleave, (1,))]
            vector_q += [(quant_u, (0, b))]
        for c in range(1, C):
            if c + 1 < C:
                vector_q += [(widen_v, a) for a in widen_on_v[c + 1]]
            vector_q += [(quant_w, (c,))]
            if c + 1 < C:
                vector_q += [(interleave, (c + 1,))]
            if c >= PROD_AFTER:
                for k in range(PROD_RATE):
                    if prod_order and prod_order[0][0] == 0:
                        vector_q.append((product, prod_order.pop(0)[1:]))
        last = {b: k for k, (s, b, c) in enumerate(prod_order) if s == 0}
        tail_q = [(product if s == 0 else accumulate, (b, c)) for s, b, c in prod_order]
        for k, op in enumerate(tail_q):
            for b in range(NB):
                if k == last[b] + GAIN_LAG[b]:
                    vector_q.append((gain, (1, b)))
                if k == last[b] + GAIN_LAG[b] + 1:
                    vector_q.append((quant_u, (1, b)))
            vector_q.append(op)

        tensor_q = [(turn_z0, (b,)) for b in range(NB)]
        adds = [(0, b, c) for c in range(C) for b in range(NB) if c < PEC[0][b]]
        for k in range(len(units) + 8):
            for b in range(NB):
                j = k - TURN_AT[b]
                if 0 <= j < PACK // TURN_GROUP[b]:
                    tensor_q += [(turn, (b, t)) for t in range(j * TURN_GROUP[b], (j + 1) * TURN_GROUP[b])]
            if k < len(units):
                tensor_q.append((mm, units[k]))
            if k >= DIAG_FROM and (k - DIAG_FROM) % DIAG_STEP == 0 and adds:
                if adds[0][2] == 0:
                    tensor_q.append((add_z0, adds[0][1:2]))
                tensor_q.append((add_scaled, adds.pop(0)))
            j = k - MM_BANKS + 1 - ADD_LAG
            if 0 <= j < len(units) and units[j][0] == 1 and units[j][2] < PEC[1][units[j][1]]:
                tensor_q.append((add_scaled, units[j]))

        issued = set()
        order = {u: k for k, u in enumerate(units)}
        f_reader = {}
        for s, b, c in units:
            f_reader[s, b, c] = (add_scaled, (s, b, c)) if c < PEC[s][b] else (product, (b, c)) if s == 0 else (accumulate, (b, c))

        def needs(fn, a):
            if fn == interleave:
                return [(widen_v if t >= PACK - WIDEN_V[a[0]] else widen_s, (a[0], t)) for t in range(PACK)]
            if fn == quant_w:
                return [(interleave, a)]
            if fn == gain:
                return [(turn_z0, (a[1],))] if a[0] == 0 else [(turn, (a[1], PACK - 1))]
            if fn == quant_u:
                return [(gain, a)]
            if fn == mm:
                k = order[a]
                r = [(quant_u, a[:2]), (quant_w, a[2:])]
                if k >= MM_BANKS:
                    r.append((tanh, units[k - MM_BANKS]))
                return r
            if fn == tanh:
                k = order[a]
                return [(mm, a)] + ([f_reader[units[k - F_TILES]]] if k >= F_TILES else [])
            if fn == product:
                return [(tanh, (0,) + a)] + ([(add_scaled, (0, a[0], PEC[0][a[0]] - 1))] if a[1] == C - 1 and PEC[0][a[0]] else [])
            if fn == accumulate:
                return [(tanh, (1,) + a)] + ([(add_scaled, (1, a[0], a[1] - 1))] if a[1] == PEC[1][a[0]] and a[1] else [])
            if fn == add_scaled:
                return [(tanh, a), (make_diag, a)]
            if fn == turn:
                return [(product, (a[0], c)) for c in range(PEC[0][a[0]], C)]
            return []

        zs_readers = []

        def bank_free(fn, a):
            reader = None
            if fn == add_z0:
                reader = (product, (a[0], C - 1))
            if fn == add_scaled and a[0] == 1 and a[2] == 0:
                reader = (accumulate, (a[1], PEC[1][a[1]]))
            if fn == turn and a[1] == 0:
                reader = (gain, (1, a[0]))
            if reader is None:
                return True
            if len(zs_readers) >= ZS_BANKS and zs_readers[-ZS_BANKS] not in issued:
                return False
            zs_readers.append(reader)
            return True

        queues = [tensor_q, scalar_q, vector_q]
        while any(queues):
            before = len(issued)
            for q in queues:
                while q and all(n in issued for n in needs(q[0][0], q[0][1])) and bank_free(*q[0]):
                    fn, a = q.pop(0)
                    fn(*a)
                    issued.add((fn, a))
            if len(issued) == before:
                raise AssertionError(f"stuck: {[(str(q[0][0]).split('.')[2][:16], q[0][1], [(str(n[0]).split('.')[2][:16],n[1]) for n in needs(*q[0]) if n not in issued]) for q in queues if q]}")
